import numpy as np
import ml_dtypes


def mxq(x, axis, fmt="e4m3"):
    dtype, down = {"e4m3": (ml_dtypes.float8_e4m3fn, 7), "e5m2": (ml_dtypes.float8_e5m2, 14)}[fmt]
    v = np.moveaxis(np.asarray(x, np.float32).astype(ml_dtypes.bfloat16).astype(np.float64), axis, -1)
    blocks = v.reshape(v.shape[:-1] + (-1, 32))
    amax = np.abs(blocks).max(-1, keepdims=True)
    byte = np.maximum(np.where(amax > 0, np.frexp(amax)[1] - 1 + 127, 0) - down, 1)
    scale = np.exp2(byte - 127.0)
    codes = (blocks / scale).astype(np.float32).astype(dtype).astype(np.float64)
    return np.moveaxis((codes * scale).reshape(v.shape), -1, axis)


WIDE = False


def mx_kscale(k, group=512):
    if not WIDE:
        return np.ones(k)
    levels = np.array([18, -18])
    if group != 512:
        return np.exp2(np.random.permutation(np.resize(levels, k // group))).repeat(group)
    if k % 512:
        return np.exp2(np.random.permutation(np.resize(levels, k // 32))).repeat(32)
    a = np.empty((k // 512, 16))
    for p in range(k // 512):
        a[p, :8] = np.random.permutation(np.resize(levels, 8))
        for g in range(8):
            far = levels[np.abs(levels - a[p, g]) >= 10]
            a[p, g + 8] = far[np.random.randint(len(far))]
    return np.exp2(a.ravel()).repeat(32)


def f64(x):
    return np.asarray(x).astype(np.float64)


def sigmoid(v):
    return 1.0 / (1.0 + np.exp(-v))


G, D, M, O, N = 4, 128, 128, 128, 512


def setup_inputs():
    n = np.random.standard_normal
    s_d = mx_kscale(D, 0)
    s_o = mx_kscale(O, 0)
    return {
        "x": (n((G, D, N)) * s_d[:, None]).astype(np.float32),
        "w1": (n((G, D, M)) / np.sqrt(D) / s_d[:, None]).astype(np.float32),
        "w2": (n((G, D, M)) / np.sqrt(D) / s_d[:, None]).astype(np.float32),
        "w3": (n((G, D, M)) / np.sqrt(D) / s_d[:, None]).astype(np.float32),
        "th": (0.5 * n((G, M, 1))).astype(np.float32),
        "wo": (n((G, O, M)) / np.sqrt(O) / s_o[:, None]).astype(np.float32),
        "dy": (n((G, O, N)) * s_o[:, None]).astype(np.float32),
        "old": (0.3 * n((G, M, N))).astype(np.float32),
    }


def reference(x, w1, w2, w3, th, wo, dy, old):
    w1q = mxq(f64(w1), 1, "e4m3")
    xq = mxq(f64(x), 1, "e4m3")
    z1 = w1q.transpose(0, 2, 1) @ xq
    w2q = mxq(f64(w2), 1, "e4m3")
    z2 = w2q.transpose(0, 2, 1) @ xq
    w3q = mxq(f64(w3), 1, "e4m3")
    z3 = w3q.transpose(0, 2, 1) @ xq
    g2 = sigmoid(z2)
    g3 = sigmoid(z3 - f64(th))
    woq = mxq(f64(wo), 1, "e4m3")
    dyq = mxq(f64(dy), 1, "e4m3")
    c0 = woq.transpose(0, 2, 1) @ dyq
    dg2 = c0 * g3 * z1
    dz2 = dg2 * g2 * (1.0 - g2)
    y = dz2 + f64(old)
    return y

@@ -1,0 +1,169 @@
+from contextlib import ExitStack
+
+import concourse.mybir as mybir
+
+G, D, M, N = 4, 128, 128, 512
+FLOPS = 4 * 2 * G * D * M * N
+
+F32 = mybir.dt.float32
+BF16 = mybir.dt.bfloat16
+U32 = mybir.dt.uint32
+U8 = mybir.dt.uint8
+FP8X4 = mybir.dt.float8_e4m3fn_x4
+ACT = mybir.ActivationFunctionType
+ALU = mybir.AluOpType
+
+P = 128
+PACK = 4
+ROWS = D // PACK
+HALF = N // 2
+MM_N = 128
+
+
+def tile_rows_btwogates_kernel(tc, x, w1, w2, w3, th, wo, dy, old, out):
+    nc = tc.nc
+    with ExitStack() as ctx:
+        sb = ctx.enter_context(tc.tile_pool(name="sb", bufs=1))
+        ps = ctx.enter_context(tc.psum_pool(name="ps", bufs=1))
+        ctx.enter_context(tc.manual_schedule())
+
+        raw, packed, codes, scales = {}, {}, {}, {}
+
+        def load(name, src, cols):
+            width = cols.stop - cols.start
+            raw[name] = sb.tile([P, PACK, width], F32, name="raw_" + name, align_bytes=64)
+            packed[name] = sb.tile([P, PACK * width], BF16, name="packed_" + name, align_bytes=64)
+            codes[name] = sb.tile([P, width], U32, name="codes_" + name, align_bytes=64)
+            scales[name] = sb.tile([P, width], U8, name="scales_" + name, align_bytes=64)
+            rows = src.rearrange("g (p j) n -> (g p) j n", j=PACK)
+            nc.sync.dma_start(out=raw[name][:], in_=rows[:, :, cols])
+
+        def interleave(copy, name, c0, c1):
+            dst = packed[name][:, PACK * c0 : PACK * c1].rearrange("p (c i j) -> p c j i", i=4, j=PACK)
+            src = raw[name][:, :, c0:c1].rearrange("p j (c i) -> p c j i", i=4)
+            copy(out=dst, in_=src)
+
+        def quantize(name):
+            nc.vector.quantize_mx(out=codes[name][:].bitcast(FP8X4), scales=scales[name][:], in_=packed[name][:])
+
+        def product(banks, place, w_name, a_name):
+            for n0 in range(0, HALF, MM_N):
+                for g in range(G):
+                    rows = slice(ROWS * g, ROWS * (g + 1))
+                    nc.tensor.matmul_mx(
+                        out=banks[g][:, place * HALF + n0 : place * HALF + n0 + MM_N],
+                        lhsT=codes[w_name][rows, :].bitcast(FP8X4),
+                        lhsT_scale=scales[w_name][rows, :],
+                        rhs=codes[a_name][rows, n0 : n0 + MM_N].bitcast(FP8X4),
+                        rhs_scale=scales[a_name][rows, n0 : n0 + MM_N],
+                        start=True,
+                        stop=True,
+                    )
+
+        gate_banks = [ps.tile([P, N], F32, name="gate_bank%d" % g) for g in range(G)]
+        value_banks = [ps.tile([P, N], F32, name="value_bank%d" % g) for g in range(G)]
+
+        def work(name):
+            return [sb.tile([P, N], F32, name="%s%d" % (name, g), align_bytes=64) for g in range(G)]
+
+        t3, t2, sq, va, vb, vh, res, prev = [work(s) for s in ("t3", "t2", "sq", "va", "vb", "vh", "res", "prev")]
+        th_sb = sb.tile([P, G], F32, name="th_sb")
+        bias3 = sb.tile([P, G], F32, name="bias3")
+
+        halves = [slice(0, HALF), slice(HALF, N)]
+        whole = slice(0, M)
+
+        with nc.allow_non_contiguous_dma(reason="one threshold a partition"):
+            nc.scalar.dma_start(out=th_sb[:], in_=th.rearrange("g m o -> m (g o)"))
+        load("w3", w3, whole)
+        load("x0", x, halves[0])
+        load("w1", w1, whole)
+        load("w2", w2, whole)
+        load("wo", wo, whole)
+        load("dy0", dy, halves[0])
+        load("x1", x, halves[1])
+        load("dy1", dy, halves[1])
+        for g in range(G):
+            nc.sync.dma_start(out=prev[g][:], in_=old[g])
+
+        def tanh3(h):
+            for g in range(G):
+                nc.scalar.activation(out=t3[g][:, halves[h]], in_=gate_banks[g][:, halves[0]], func=ACT.Tanh,
+                                     scale=0.5, bias=bias3[:, g : g + 1])
+
+        def tanh2(h):
+            for g in range(G):
+                nc.scalar.activation(out=t2[g][:, halves[h]], in_=gate_banks[g][:, halves[1]], func=ACT.Tanh, scale=0.5)
+
+        def square2(h):
+            for g in range(G):
+                nc.scalar.activation(out=sq[g][:, halves[h]], in_=t2[g][:, halves[h]], func=ACT.Square)
+
+        def times_z1(h, groups):
+            for g in groups:
+                nc.vector.scalar_tensor_tensor(out=va[g][:, halves[h]], in0=t3[g][:, halves[h]], scalar=1.0,
+                                               in1=value_banks[g][:, halves[0]], op0=ALU.add, op1=ALU.mult)
+
+        def times_c0(h, groups):
+            for g in groups:
+                nc.vector.scalar_tensor_tensor(out=vb[g][:, halves[h]], in0=va[g][:, halves[h]], scalar=-0.125,
+                                               in1=value_banks[g][:, halves[1]], op0=ALU.mult, op1=ALU.mult)
+
+        def times_slope(h, groups):
+            for g in groups:
+                nc.vector.scalar_tensor_tensor(out=vh[g][:, halves[h]], in0=sq[g][:, halves[h]], scalar=1.0,
+                                               in1=vb[g][:, halves[h]], op0=ALU.subtract, op1=ALU.mult)
+
+        def add_old(h, groups):
+            for g in groups:
+                nc.vector.tensor_tensor(out=res[g][:, halves[h]], in0=vh[g][:, halves[h]], in1=prev[g][:, halves[h]],
+                                        op=ALU.add)
+                nc.sync.dma_start(out=out[g, :, halves[h]], in_=res[g][:, halves[h]])
+
+        every = range(G)
+        v_copy, s_copy = nc.vector.tensor_copy, nc.scalar.copy
+
+        nc.scalar.activation(out=bias3[:], in_=th_sb[:], func=ACT.Copy, scale=-0.5)
+        interleave(v_copy, "w3", 0, M)
+        quantize("w3")
+        interleave(v_copy, "x0", 0, 160)
+        interleave(s_copy, "x0", 160, HALF)
+        quantize("x0")
+        product(gate_banks, 0, "w3", "x0")
+        interleave(s_copy, "w1", 0, M)
+        quantize("w1")
+        product(value_banks, 0, "w1", "x0")
+        interleave(s_copy, "w2", 0, M)
+        quantize("w2")
+        tanh3(0)
+        product(gate_banks, 1, "w2", "x0")
+        interleave(v_copy, "wo", 0, M)
+        times_z1(0, [0])
+        quantize("wo")
+        times_z1(0, [1, 2])
+        interleave(s_copy, "dy0", 128, HALF)
+        interleave(v_copy, "dy0", 0, 128)
+        times_z1(0, [3])
+        quantize("dy0")
+        product(value_banks, 1, "wo", "dy0")
+        tanh2(0)
+        interleave(v_copy, "x1", 0, HALF)
+        times_c0(0, [0])
+        quantize("x1")
+        product(gate_banks, 0, "w3", "x1")
+        square2(0)
+        times_c0(0, [1, 2, 3])
+        product(value_banks, 0, "w1", "x1")
+        interleave(s_copy, "dy1", 0, HALF)
+        tanh3(1)
+        product(gate_banks, 1, "w2", "x1")
+        times_slope(0, every)
+        quantize("dy1")
+        add_old(0, every)
+        tanh2(1)
+        square2(1)
+        times_z1(1, every)
+        product(value_banks, 1, "wo", "dy1")
+        times_c0(1, every)
+        times_slope(1, every)
+        add_old(1, every)

@@ -46,124 +46,146 @@ def tile_rows_btwogates_kernel(tc, x, w1, w2, w3, th, wo, dy, old, out):
         def quantize(name):
             nc.vector.quantize_mx(out=codes[name][:].bitcast(FP8X4), scales=scales[name][:], in_=packed[name][:])
 
-        def product(banks, place, w_name, a_name):
-            for n0 in range(0, HALF, MM_N):
-                for g in range(G):
-                    rows = slice(ROWS * g, ROWS * (g + 1))
-                    nc.tensor.matmul_mx(
-                        out=banks[g][:, place * HALF + n0 : place * HALF + n0 + MM_N],
-                        lhsT=codes[w_name][rows, :].bitcast(FP8X4),
-                        lhsT_scale=scales[w_name][rows, :],
-                        rhs=codes[a_name][rows, n0 : n0 + MM_N].bitcast(FP8X4),
-                        rhs_scale=scales[a_name][rows, n0 : n0 + MM_N],
-                        start=True,
-                        stop=True,
-                    )
+        def product(banks, place, w_name, w_cols, a_name, order):
+            for g, n0 in order:
+                rows = slice(ROWS * g, ROWS * (g + 1))
+                nc.tensor.matmul_mx(
+                    out=banks[g][:, place * HALF + n0 : place * HALF + n0 + MM_N],
+                    lhsT=codes[w_name][rows, w_cols].bitcast(FP8X4),
+                    lhsT_scale=scales[w_name][rows, w_cols],
+                    rhs=codes[a_name][rows, n0 : n0 + MM_N].bitcast(FP8X4),
+                    rhs_scale=scales[a_name][rows, n0 : n0 + MM_N],
+                    start=True,
+                    stop=True,
+                )
+
+        across = [(g, n0) for n0 in range(0, HALF, MM_N) for g in range(G)]
+        by_group = [(g, n0) for g in range(G) for n0 in range(0, HALF, MM_N)]
 
         gate_banks = [ps.tile([P, N], F32, name="gate_bank%d" % g) for g in range(G)]
         value_banks = [ps.tile([P, N], F32, name="value_bank%d" % g) for g in range(G)]
 
-        def work(name):
-            return [sb.tile([P, N], F32, name="%s%d" % (name, g), align_bytes=64) for g in range(G)]
+        def work(name, shape):
+            return [[sb.tile(shape, F32, name="%s%d%d" % (name, h, pair), align_bytes=64) for pair in range(2)] for h in range(2)]
 
-        t3, t2, sq, va, vb, vh, res, prev = [work(s) for s in ("t3", "t2", "sq", "va", "vb", "vh", "res", "prev")]
-        th_sb = sb.tile([P, G], F32, name="th_sb")
+        t2 = work("t2", [P, 2, HALF])
+        gates = work("gates", [P, 2, 2, HALF])
+        parts = work("parts", [P, 2, 2, HALF])
+        grad = work("grad", [P, 2, HALF])
+        res = work("res", [P, 2, HALF])
+        prev = [sb.tile([P, 2, N], F32, name="prev%d" % pair, align_bytes=64) for pair in range(2)]
+        th_rows = sb.tile([P, P], F32, name="th_rows", align_bytes=64)
+        th_cols = sb.tile([P, P], F32, name="th_cols", align_bytes=64)
         bias3 = sb.tile([P, G], F32, name="bias3")
 
         halves = [slice(0, HALF), slice(HALF, N)]
         whole = slice(0, M)
 
-        with nc.allow_non_contiguous_dma(reason="one threshold a partition"):
-            nc.scalar.dma_start(out=th_sb[:], in_=th.rearrange("g m o -> m (g o)"))
-        load("w3", w3, whole)
+        nc.vector.memset(th_rows[:], 0.0)
         load("x0", x, halves[0])
-        load("w1", w1, whole)
+        nc.sync.dma_start(out=th_rows[0:P:ROWS, :].rearrange("c (g i) -> c g i", g=G),
+                          in_=th.rearrange("g (c i) o -> c g (i o)", c=G))
         load("w2", w2, whole)
-        load("wo", wo, whole)
+        load("w3", w3, whole)
         load("dy0", dy, halves[0])
+        load("wo", wo, whole)
+        load("w1", w1, whole)
         load("x1", x, halves[1])
         load("dy1", dy, halves[1])
-        for g in range(G):
-            nc.sync.dma_start(out=prev[g][:], in_=old[g])
+        for pair in range(2):
+            nc.sync.dma_start(out=prev[pair][:], in_=old[2 * pair : 2 * pair + 2].rearrange("g m n -> m g n"))
 
-        def tanh3(h):
-            for g in range(G):
-                nc.scalar.activation(out=t3[g][:, halves[h]], in_=gate_banks[g][:, halves[0]], func=ACT.Tanh,
-                                     scale=0.5, bias=bias3[:, g : g + 1])
+        def tanh3(h, g):
+            nc.scalar.activation(out=gates[h][g // 2][:, g % 2, 0, :], in_=gate_banks[g][:, halves[0]], func=ACT.Tanh,
+                                 scale=-0.5, bias=bias3[:, g : g + 1])
 
-        def tanh2(h):
-            for g in range(G):
-                nc.scalar.activation(out=t2[g][:, halves[h]], in_=gate_banks[g][:, halves[1]], func=ACT.Tanh, scale=0.5)
+        def tanh2(h, g):
+            nc.scalar.activation(out=t2[h][g // 2][:, g % 2, :], in_=gate_banks[g][:, halves[1]], func=ACT.Tanh, scale=0.5)
 
-        def square2(h):
-            for g in range(G):
-                nc.scalar.activation(out=sq[g][:, halves[h]], in_=t2[g][:, halves[h]], func=ACT.Square)
+        def square2(h, pair):
+            nc.scalar.activation(out=gates[h][pair][:, :, 1, :], in_=t2[h][pair][:], func=ACT.Square)
 
-        def times_z1(h, groups):
-            for g in groups:
-                nc.vector.scalar_tensor_tensor(out=va[g][:, halves[h]], in0=t3[g][:, halves[h]], scalar=1.0,
-                                               in1=value_banks[g][:, halves[0]], op0=ALU.add, op1=ALU.mult)
+        def gate_values(h, g):
+            nc.vector.scalar_tensor_tensor(out=parts[h][g // 2][:, g % 2].rearrange("p a n -> p (a n)"),
+                                           in0=gates[h][g // 2][:, g % 2].rearrange("p a n -> p (a n)"), scalar=1.0,
+                                           in1=value_banks[g][:], op0=ALU.subtract, op1=ALU.mult)
 
-        def times_c0(h, groups):
-            for g in groups:
-                nc.vector.scalar_tensor_tensor(out=vb[g][:, halves[h]], in0=va[g][:, halves[h]], scalar=-0.125,
-                                               in1=value_banks[g][:, halves[1]], op0=ALU.mult, op1=ALU.mult)
+        def join(h, pair, members):
+            nc.vector.scalar_tensor_tensor(out=grad[h][pair][:, members, :], in0=parts[h][pair][:, members, 0, :], scalar=0.125,
+                                           in1=parts[h][pair][:, members, 1, :], op0=ALU.mult, op1=ALU.mult)
 
-        def times_slope(h, groups):
-            for g in groups:
-                nc.vector.scalar_tensor_tensor(out=vh[g][:, halves[h]], in0=sq[g][:, halves[h]], scalar=1.0,
-                                               in1=vb[g][:, halves[h]], op0=ALU.subtract, op1=ALU.mult)
+        def add_old(engine, h, pair, members):
+            engine.tensor_tensor(out=res[h][pair][:, members, :], in0=grad[h][pair][:, members, :],
+                                 in1=prev[pair][:, members, halves[h]], op=ALU.add)
+            dst = out[2 * pair : 2 * pair + 2].rearrange("g m n -> m g n")
+            nc.sync.dma_start(out=dst[:, members, halves[h]], in_=res[h][pair][:, members, :])
 
-        def add_old(h, groups):
-            for g in groups:
-                nc.vector.tensor_tensor(out=res[g][:, halves[h]], in0=vh[g][:, halves[h]], in1=prev[g][:, halves[h]],
-                                        op=ALU.add)
-                nc.sync.dma_start(out=out[g, :, halves[h]], in_=res[g][:, halves[h]])
+        both = slice(0, 2)
+        v_copy = nc.vector.tensor_copy
 
-        every = range(G)
-        v_copy, s_copy = nc.vector.tensor_copy, nc.scalar.copy
+        def s_copy(out, in_):
+            nc.scalar.activation(out=out, in_=in_, func=ACT.Copy)
 
-        nc.scalar.activation(out=bias3[:], in_=th_sb[:], func=ACT.Copy, scale=-0.5)
-        interleave(v_copy, "w3", 0, M)
-        quantize("w3")
+
         interleave(v_copy, "x0", 0, 160)
         interleave(s_copy, "x0", 160, HALF)
+        interleave(v_copy, "w2", 0, M)
         quantize("x0")
-        product(gate_banks, 0, "w3", "x0")
-        interleave(s_copy, "w1", 0, M)
-        quantize("w1")
-        product(value_banks, 0, "w1", "x0")
-        interleave(s_copy, "w2", 0, M)
         quantize("w2")
-        tanh3(0)
-        product(gate_banks, 1, "w2", "x0")
+        product(gate_banks, 1, "w2", whole, "x0", across)
+        nc.vector.transpose(out=th_cols[:], in_=th_rows[:])
+        interleave(s_copy, "w3", 0, M)
+        nc.scalar.activation(out=bias3[:], in_=th_cols[:, 0:P:ROWS], func=ACT.Copy, scale=0.5)
+        quantize("w3")
+        for g in range(3):
+            tanh2(0, g)
+        square2(0, 0)
+        interleave(v_copy, "dy0", 0, HALF)
         interleave(v_copy, "wo", 0, M)
-        times_z1(0, [0])
-        quantize("wo")
-        times_z1(0, [1, 2])
-        interleave(s_copy, "dy0", 128, HALF)
-        interleave(v_copy, "dy0", 0, 128)
-        times_z1(0, [3])
         quantize("dy0")
-        product(value_banks, 1, "wo", "dy0")
-        tanh2(0)
+        interleave(v_copy, "w1", 0, M)
+        quantize("wo")
+        quantize("w1")
+        product(gate_banks, 0, "w3", whole, "x0", by_group[:6])
+        tanh3(0, 0)
+        tanh3(0, 1)
+        tanh2(0, 3)
+        product(value_banks, 1, "wo", whole, "dy0", across)
+        product(value_banks, 0, "w1", whole, "x0", across)
+        product(gate_banks, 0, "w3", whole, "x0", by_group[6:])
+        tanh3(0, 2)
+        square2(0, 1)
+        tanh3(0, 3)
         interleave(v_copy, "x1", 0, HALF)
-        times_c0(0, [0])
+        gate_values(0, 0)
         quantize("x1")
-        product(gate_banks, 0, "w3", "x1")
-        square2(0)
-        times_c0(0, [1, 2, 3])
-        product(value_banks, 0, "w1", "x1")
+        for g in range(G):
+            product(gate_banks, 1, "w2", whole, "x1", by_group[2 * g : 2 * g + 2])
+            product(gate_banks, 0, "w3", whole, "x1", by_group[2 * g : 2 * g + 2])
         interleave(s_copy, "dy1", 0, HALF)
-        tanh3(1)
-        product(gate_banks, 1, "w2", "x1")
-        times_slope(0, every)
+        gate_values(0, 1)
+        join(0, 0, both)
+        add_old(nc.gpsimd, 0, 0, both)
+        gate_values(0, 2)
+        gate_values(0, 3)
         quantize("dy1")
-        add_old(0, every)
-        tanh2(1)
-        square2(1)
-        times_z1(1, every)
-        product(value_banks, 1, "wo", "dy1")
-        times_c0(1, every)
-        times_slope(1, every)
-        add_old(1, every)
+        product(value_banks, 0, "w1", whole, "x1", by_group)
+        product(value_banks, 1, "wo", whole, "dy1", across)
+        join(0, 1, both)
+        add_old(nc.gpsimd, 0, 1, both)
+        for pair in range(2):
+            tanh2(1, 2 * pair)
+            tanh2(1, 2 * pair + 1)
+            tanh3(1, 2 * pair)
+            square2(1, pair)
+            tanh3(1, 2 * pair + 1)
+        gate_values(1, 0)
+        gate_values(1, 1)
+        join(1, 0, both)
+        add_old(nc.gpsimd, 1, 0, both)
+        gate_values(1, 2)
+        gate_values(1, 3)
+        join(1, 1, slice(0, 1))
+        join(1, 1, slice(1, 2))
+        add_old(nc.vector, 1, 1, slice(0, 1))
+        add_old(nc.vector, 1, 1, slice(1, 2))

@@ -46,21 +46,18 @@ def tile_rows_btwogates_kernel(tc, x, w1, w2, w3, th, wo, dy, old, out):
         def quantize(name):
             nc.vector.quantize_mx(out=codes[name][:].bitcast(FP8X4), scales=scales[name][:], in_=packed[name][:])
 
-        def product(banks, place, w_name, w_cols, a_name, order):
-            for g, n0 in order:
-                rows = slice(ROWS * g, ROWS * (g + 1))
+        def product(banks, place, w_name, a_name, g):
+            rows = slice(ROWS * g, ROWS * (g + 1))
+            for n0 in range(0, HALF, MM_N):
                 nc.tensor.matmul_mx(
                     out=banks[g][:, place * HALF + n0 : place * HALF + n0 + MM_N],
-                    lhsT=codes[w_name][rows, w_cols].bitcast(FP8X4),
-                    lhsT_scale=scales[w_name][rows, w_cols],
+                    lhsT=codes[w_name][rows, :].bitcast(FP8X4),
+                    lhsT_scale=scales[w_name][rows, :],
                     rhs=codes[a_name][rows, n0 : n0 + MM_N].bitcast(FP8X4),
                     rhs_scale=scales[a_name][rows, n0 : n0 + MM_N],
                     start=True,
                     stop=True,
                 )
-
-        across = [(g, n0) for n0 in range(0, HALF, MM_N) for g in range(G)]
-        by_group = [(g, n0) for g in range(G) for n0 in range(0, HALF, MM_N)]
 
         gate_banks = [ps.tile([P, N], F32, name="gate_bank%d" % g) for g in range(G)]
         value_banks = [ps.tile([P, N], F32, name="value_bank%d" % g) for g in range(G)]
@@ -127,51 +124,66 @@ def tile_rows_btwogates_kernel(tc, x, w1, w2, w3, th, wo, dy, old, out):
             nc.scalar.activation(out=out, in_=in_, func=ACT.Copy)
 
 
+        def gate_products(h, g):
+            product(gate_banks, 1, "w2", "x%d" % h, g)
+            product(gate_banks, 0, "w3", "x%d" % h, g)
+
+        def value_products(h, g):
+            product(value_banks, 1, "wo", "dy%d" % h, g)
+            product(value_banks, 0, "w1", "x%d" % h, g)
+
+        first, second = slice(0, 1), slice(1, 2)
         interleave(v_copy, "x0", 0, 160)
         interleave(s_copy, "x0", 160, HALF)
         interleave(v_copy, "w2", 0, M)
         quantize("x0")
         quantize("w2")
-        product(gate_banks, 1, "w2", whole, "x0", across)
+        for g in range(G):
+            product(gate_banks, 1, "w2", "x0", g)
         nc.vector.transpose(out=th_cols[:], in_=th_rows[:])
         interleave(s_copy, "w3", 0, M)
         nc.scalar.activation(out=bias3[:], in_=th_cols[:, 0:P:ROWS], func=ACT.Copy, scale=0.5)
         quantize("w3")
         for g in range(3):
             tanh2(0, g)
+            product(gate_banks, 0, "w3", "x0", g)
         square2(0, 0)
+        tanh2(0, 3)
+        product(gate_banks, 0, "w3", "x0", 3)
         interleave(v_copy, "dy0", 0, HALF)
         interleave(v_copy, "wo", 0, M)
         quantize("dy0")
         interleave(v_copy, "w1", 0, M)
         quantize("wo")
         quantize("w1")
-        product(gate_banks, 0, "w3", whole, "x0", by_group[:6])
+        for g in range(G):
+            value_products(0, g)
         tanh3(0, 0)
         tanh3(0, 1)
-        tanh2(0, 3)
-        product(value_banks, 1, "wo", whole, "dy0", across)
-        product(value_banks, 0, "w1", whole, "x0", across)
-        product(gate_banks, 0, "w3", whole, "x0", by_group[6:])
-        tanh3(0, 2)
         square2(0, 1)
+        interleave(s_copy, "dy1", 0, HALF)
+        tanh3(0, 2)
         tanh3(0, 3)
         interleave(v_copy, "x1", 0, HALF)
         gate_values(0, 0)
         quantize("x1")
-        for g in range(G):
-            product(gate_banks, 1, "w2", whole, "x1", by_group[2 * g : 2 * g + 2])
-            product(gate_banks, 0, "w3", whole, "x1", by_group[2 * g : 2 * g + 2])
-        interleave(s_copy, "dy1", 0, HALF)
+        gate_products(1, 0)
+        gate_products(1, 1)
         gate_values(0, 1)
-        join(0, 0, both)
+        join(0, 0, first)
+        quantize("dy1")
+        value_products(1, 0)
+        gate_products(1, 2)
+        value_products(1, 1)
+        gate_products(1, 3)
+        join(0, 0, second)
         add_old(nc.gpsimd, 0, 0, both)
         gate_values(0, 2)
         gate_values(0, 3)
-        quantize("dy1")
-        product(value_banks, 0, "w1", whole, "x1", by_group)
-        product(value_banks, 1, "wo", whole, "dy1", across)
-        join(0, 1, both)
+        value_products(1, 2)
+        value_products(1, 3)
+        join(0, 1, first)
+        join(0, 1, second)
         add_old(nc.gpsimd, 0, 1, both)
         for pair in range(2):
             tanh2(1, 2 * pair)
@@ -181,11 +193,12 @@ def tile_rows_btwogates_kernel(tc, x, w1, w2, w3, th, wo, dy, old, out):
             tanh3(1, 2 * pair + 1)
         gate_values(1, 0)
         gate_values(1, 1)
-        join(1, 0, both)
+        join(1, 0, first)
+        join(1, 0, second)
         add_old(nc.gpsimd, 1, 0, both)
         gate_values(1, 2)
         gate_values(1, 3)
-        join(1, 1, slice(0, 1))
-        join(1, 1, slice(1, 2))
-        add_old(nc.vector, 1, 1, slice(0, 1))
-        add_old(nc.vector, 1, 1, slice(1, 2))
+        join(1, 1, first)
+        join(1, 1, second)
+        add_old(nc.vector, 1, 1, first)
+        add_old(nc.vector, 1, 1, second)

@@ -29,26 +29,26 @@ def tile_rows_btwogates_kernel(tc, x, w1, w2, w3, th, wo, dy, old, out):
 
         raw, packed, codes, scales = {}, {}, {}, {}
 
-        def load(name, src, cols):
-            width = cols.stop - cols.start
-            raw[name] = sb.tile([P, PACK, width], F32, name="raw_" + name, align_bytes=64)
+        def load(name, src):
+            raw[name] = sb.tile([P, PACK, src.shape[2]], F32, name="raw_" + name, align_bytes=64)
+            nc.sync.dma_start(out=raw[name][:], in_=src.rearrange("g (p j) n -> (g p) j n", j=PACK))
+
+        def operand(name, width):
             packed[name] = sb.tile([P, PACK * width], BF16, name="packed_" + name, align_bytes=64)
             codes[name] = sb.tile([P, width], U32, name="codes_" + name, align_bytes=64)
             scales[name] = sb.tile([P, width], U8, name="scales_" + name, align_bytes=64)
-            rows = src.rearrange("g (p j) n -> (g p) j n", j=PACK)
-            nc.sync.dma_start(out=raw[name][:], in_=rows[:, :, cols])
 
-        def interleave(copy, name, c0, c1):
+        def interleave(copy, name, src_name, src0, c0, c1):
             dst = packed[name][:, PACK * c0 : PACK * c1].rearrange("p (c i j) -> p c j i", i=4, j=PACK)
-            src = raw[name][:, :, c0:c1].rearrange("p j (c i) -> p c j i", i=4)
+            src = raw[src_name][:, :, src0 + c0 : src0 + c1].rearrange("p j (c i) -> p c j i", i=4)
             copy(out=dst, in_=src)
 
         def quantize(name):
             nc.vector.quantize_mx(out=codes[name][:].bitcast(FP8X4), scales=scales[name][:], in_=packed[name][:])
 
-        def product(banks, place, w_name, a_name, g):
+        def product(banks, place, w_name, a_name, g, starts):
             rows = slice(ROWS * g, ROWS * (g + 1))
-            for n0 in range(0, HALF, MM_N):
+            for n0 in starts:
                 nc.tensor.matmul_mx(
                     out=banks[g][:, place * HALF + n0 : place * HALF + n0 + MM_N],
                     lhsT=codes[w_name][rows, :].bitcast(FP8X4),
@@ -76,19 +76,20 @@ def tile_rows_btwogates_kernel(tc, x, w1, w2, w3, th, wo, dy, old, out):
         bias3 = sb.tile([P, G], F32, name="bias3")
 
         halves = [slice(0, HALF), slice(HALF, N)]
-        whole = slice(0, M)
 
         nc.vector.memset(th_rows[:], 0.0)
-        load("x0", x, halves[0])
+        load("x", x)
         nc.sync.dma_start(out=th_rows[0:P:ROWS, :].rearrange("c (g i) -> c g i", g=G),
                           in_=th.rearrange("g (c i) o -> c g (i o)", c=G))
-        load("w2", w2, whole)
-        load("w3", w3, whole)
-        load("dy0", dy, halves[0])
-        load("wo", wo, whole)
-        load("w1", w1, whole)
-        load("x1", x, halves[1])
-        load("dy1", dy, halves[1])
+        load("w3", w3)
+        load("w1", w1)
+        load("w2", w2)
+        load("dy", dy)
+        load("wo", wo)
+        for name in ("w1", "w2", "w3", "wo"):
+            operand(name, M)
+        for name in ("x0", "x1", "dy0", "dy1"):
+            operand(name, HALF)
         for pair in range(2):
             nc.sync.dma_start(out=prev[pair][:], in_=old[2 * pair : 2 * pair + 2].rearrange("g m n -> m g n"))
 
@@ -124,67 +125,80 @@ def tile_rows_btwogates_kernel(tc, x, w1, w2, w3, th, wo, dy, old, out):
             nc.scalar.activation(out=out, in_=in_, func=ACT.Copy)
 
 
+        def across(banks, place, w_name, a_name):
+            for n0 in range(0, HALF, MM_N):
+                for g in range(G):
+                    product(banks, place, w_name, a_name, g, [n0])
+
         def gate_products(h, g):
-            product(gate_banks, 1, "w2", "x%d" % h, g)
-            product(gate_banks, 0, "w3", "x%d" % h, g)
+            product(gate_banks, 1, "w2", "x%d" % h, g, blocks)
+            product(gate_banks, 0, "w3", "x%d" % h, g, blocks)
 
         def value_products(h, g):
-            product(value_banks, 1, "wo", "dy%d" % h, g)
-            product(value_banks, 0, "w1", "x%d" % h, g)
+            product(value_banks, 0, "w1", "x%d" % h, g, blocks)
+            product(value_banks, 1, "wo", "dy%d" % h, g, blocks)
 
+        def times_z1(g):
+            nc.vector.scalar_tensor_tensor(out=parts[0][g // 2][:, g % 2, 0, :], in0=gates[0][g // 2][:, g % 2, 0, :], scalar=1.0,
+                                           in1=value_banks[g][:, halves[0]], op0=ALU.subtract, op1=ALU.mult)
+
+        def times_slope(pair):
+            nc.vector.scalar_tensor_tensor(out=parts[0][pair][:, :, 1, :], in0=gates[0][pair][:, :, 1, :], scalar=1.0,
+                                           in1=parts[0][pair][:, :, 0, :], op0=ALU.subtract, op1=ALU.mult)
+
+        def times_c0(g):
+            nc.vector.scalar_tensor_tensor(out=grad[0][g // 2][:, g % 2, :], in0=parts[0][g // 2][:, g % 2, 1, :], scalar=0.125,
+                                           in1=value_banks[g][:, halves[1]], op0=ALU.mult, op1=ALU.mult)
+
+        blocks = list(range(0, HALF, MM_N))
         first, second = slice(0, 1), slice(1, 2)
-        interleave(v_copy, "x0", 0, 160)
-        interleave(s_copy, "x0", 160, HALF)
-        interleave(v_copy, "w2", 0, M)
+        interleave(v_copy, "x0", "x", 0, 0, HALF)
+        interleave(s_copy, "x1", "x", HALF, 0, HALF)
+        interleave(v_copy, "w3", "w3", 0, 0, M)
         quantize("x0")
+        quantize("w3")
+        across(gate_banks, 0, "w3", "x0")
+        nc.vector.transpose(out=th_cols[:], in_=th_rows[:])
+        interleave(s_copy, "w1", "w1", 0, 0, M)
+        nc.scalar.activation(out=bias3[:], in_=th_cols[:, 0:P:ROWS], func=ACT.Copy, scale=0.5)
+        quantize("x1")
+        quantize("w1")
+        across(value_banks, 0, "w1", "x0")
+        interleave(v_copy, "w2", "w2", 0, 0, M)
         quantize("w2")
         for g in range(G):
-            product(gate_banks, 1, "w2", "x0", g)
-        nc.vector.transpose(out=th_cols[:], in_=th_rows[:])
-        interleave(s_copy, "w3", 0, M)
-        nc.scalar.activation(out=bias3[:], in_=th_cols[:, 0:P:ROWS], func=ACT.Copy, scale=0.5)
-        quantize("w3")
+            tanh3(0, g)
+            product(gate_banks, 1, "w2", "x0", g, blocks)
         for g in range(3):
+            times_z1(g)
             tanh2(0, g)
-            product(gate_banks, 0, "w3", "x0", g)
         square2(0, 0)
         tanh2(0, 3)
-        product(gate_banks, 0, "w3", "x0", 3)
-        interleave(v_copy, "dy0", 0, HALF)
-        interleave(v_copy, "wo", 0, M)
+        interleave(v_copy, "dy0", "dy", 0, 0, HALF)
+        times_z1(3)
+        interleave(v_copy, "wo", "wo", 0, 0, M)
         quantize("dy0")
-        interleave(v_copy, "w1", 0, M)
         quantize("wo")
-        quantize("w1")
-        for g in range(G):
-            value_products(0, g)
-        tanh3(0, 0)
-        tanh3(0, 1)
+        for g in range(3):
+            gate_products(1, g)
+        across(value_banks, 1, "wo", "dy0")
+        gate_products(1, 3)
+        interleave(s_copy, "dy1", "dy", HALF, 0, HALF // 2)
         square2(0, 1)
-        interleave(s_copy, "dy1", 0, HALF)
-        tanh3(0, 2)
-        tanh3(0, 3)
-        interleave(v_copy, "x1", 0, HALF)
-        gate_values(0, 0)
-        quantize("x1")
-        gate_products(1, 0)
-        gate_products(1, 1)
-        gate_values(0, 1)
-        join(0, 0, first)
+        interleave(s_copy, "dy1", "dy", HALF, HALF // 2, 3 * HALF // 4)
+        times_slope(0)
+        interleave(v_copy, "dy1", "dy", HALF, 3 * HALF // 4, HALF)
+        times_c0(0)
+        times_slope(1)
         quantize("dy1")
         value_products(1, 0)
-        gate_products(1, 2)
-        value_products(1, 1)
-        gate_products(1, 3)
-        join(0, 0, second)
+        times_c0(1)
         add_old(nc.gpsimd, 0, 0, both)
-        gate_values(0, 2)
-        gate_values(0, 3)
+        value_products(1, 1)
+        times_c0(2)
+        times_c0(3)
         value_products(1, 2)
         value_products(1, 3)
-        join(0, 1, first)
-        join(0, 1, second)
-        add_old(nc.gpsimd, 0, 1, both)
         for pair in range(2):
             tanh2(1, 2 * pair)
             tanh2(1, 2 * pair + 1)
@@ -192,9 +206,11 @@ def tile_rows_btwogates_kernel(tc, x, w1, w2, w3, th, wo, dy, old, out):
             square2(1, pair)
             tanh3(1, 2 * pair + 1)
         gate_values(1, 0)
+        add_old(nc.gpsimd, 0, 1, first)
         gate_values(1, 1)
         join(1, 0, first)
         join(1, 0, second)
+        add_old(nc.vector, 0, 1, second)
         add_old(nc.gpsimd, 1, 0, both)
         gate_values(1, 2)
         gate_values(1, 3)

@@ -18,6 +18,8 @@ PACK = 4
 ROWS = D // PACK
 HALF = N // 2
 MM_N = 128
+LINE = 4
+DY1_SPLIT = 3 * HALF // 4
 
 
 def tile_rows_btwogates_kernel(tc, x, w1, w2, w3, th, wo, dy, old, out):
@@ -38,32 +40,36 @@ def tile_rows_btwogates_kernel(tc, x, w1, w2, w3, th, wo, dy, old, out):
             codes[name] = sb.tile([P, width], U32, name="codes_" + name, align_bytes=64)
             scales[name] = sb.tile([P, width], U8, name="scales_" + name, align_bytes=64)
 
-        def interleave(copy, name, src_name, src0, c0, c1):
-            dst = packed[name][:, PACK * c0 : PACK * c1].rearrange("p (c i j) -> p c j i", i=4, j=PACK)
-            src = raw[src_name][:, :, src0 + c0 : src0 + c1].rearrange("p j (c i) -> p c j i", i=4)
+        def interleave(copy, name, src_name, src0, start, stop):
+            dst = packed[name][:, PACK * start : PACK * stop].rearrange("p (c i j) -> p c j i", i=LINE, j=PACK)
+            src = raw[src_name][:, :, src0 + start : src0 + stop].rearrange("p j (c i) -> p c j i", i=LINE)
             copy(out=dst, in_=src)
 
         def quantize(name):
             nc.vector.quantize_mx(out=codes[name][:].bitcast(FP8X4), scales=scales[name][:], in_=packed[name][:])
 
-        def product(banks, place, w_name, a_name, g, starts):
-            rows = slice(ROWS * g, ROWS * (g + 1))
-            for n0 in starts:
-                nc.tensor.matmul_mx(
-                    out=banks[g][:, place * HALF + n0 : place * HALF + n0 + MM_N],
-                    lhsT=codes[w_name][rows, :].bitcast(FP8X4),
-                    lhsT_scale=scales[w_name][rows, :],
-                    rhs=codes[a_name][rows, n0 : n0 + MM_N].bitcast(FP8X4),
-                    rhs_scale=scales[a_name][rows, n0 : n0 + MM_N],
-                    start=True,
-                    stop=True,
-                )
+        def multiply(jobs):
+            for n0 in range(0, HALF, MM_N):
+                for banks, place, w_name, a_name, g in jobs:
+                    rows = slice(ROWS * g, ROWS * (g + 1))
+                    nc.tensor.matmul_mx(
+                        out=banks[g][:, place * HALF + n0 : place * HALF + n0 + MM_N],
+                        lhsT=codes[w_name][rows, :].bitcast(FP8X4),
+                        lhsT_scale=scales[w_name][rows, :],
+                        rhs=codes[a_name][rows, n0 : n0 + MM_N].bitcast(FP8X4),
+                        rhs_scale=scales[a_name][rows, n0 : n0 + MM_N],
+                        start=True,
+                        stop=True,
+                    )
 
         gate_banks = [ps.tile([P, N], F32, name="gate_bank%d" % g) for g in range(G)]
         value_banks = [ps.tile([P, N], F32, name="value_bank%d" % g) for g in range(G)]
 
         def work(name, shape):
-            return [[sb.tile(shape, F32, name="%s%d%d" % (name, h, pair), align_bytes=64) for pair in range(2)] for h in range(2)]
+            return [
+                [sb.tile(shape, F32, name="%s%d%d" % (name, h, pair), align_bytes=64) for pair in range(2)]
+                for h in range(2)
+            ]
 
         t2 = work("t2", [P, 2, HALF])
         gates = work("gates", [P, 2, 2, HALF])
@@ -79,8 +85,10 @@ def tile_rows_btwogates_kernel(tc, x, w1, w2, w3, th, wo, dy, old, out):
 
         nc.vector.memset(th_rows[:], 0.0)
         load("x", x)
-        nc.sync.dma_start(out=th_rows[0:P:ROWS, :].rearrange("c (g i) -> c g i", g=G),
-                          in_=th.rearrange("g (c i) o -> c g (i o)", c=G))
+        nc.sync.dma_start(
+            out=th_rows[0:P:ROWS, :].rearrange("c (g i) -> c g i", g=G),
+            in_=th.rearrange("g (c i) o -> c g (i o)", c=G),
+        )
         load("w3", w3)
         load("w1", w1)
         load("w2", w2)
@@ -94,127 +102,150 @@ def tile_rows_btwogates_kernel(tc, x, w1, w2, w3, th, wo, dy, old, out):
             nc.sync.dma_start(out=prev[pair][:], in_=old[2 * pair : 2 * pair + 2].rearrange("g m n -> m g n"))
 
         def tanh3(h, g):
-            nc.scalar.activation(out=gates[h][g // 2][:, g % 2, 0, :], in_=gate_banks[g][:, halves[0]], func=ACT.Tanh,
-                                 scale=-0.5, bias=bias3[:, g : g + 1])
+            nc.scalar.activation(
+                out=gates[h][g // 2][:, g % 2, 0, :],
+                in_=gate_banks[g][:, halves[0]],
+                func=ACT.Tanh,
+                scale=-0.5,
+                bias=bias3[:, g : g + 1],
+            )
 
         def tanh2(h, g):
-            nc.scalar.activation(out=t2[h][g // 2][:, g % 2, :], in_=gate_banks[g][:, halves[1]], func=ACT.Tanh, scale=0.5)
+            nc.scalar.activation(
+                out=t2[h][g // 2][:, g % 2, :], in_=gate_banks[g][:, halves[1]], func=ACT.Tanh, scale=0.5
+            )
 
         def square2(h, pair):
             nc.scalar.activation(out=gates[h][pair][:, :, 1, :], in_=t2[h][pair][:], func=ACT.Square)
 
-        def gate_values(h, g):
-            nc.vector.scalar_tensor_tensor(out=parts[h][g // 2][:, g % 2].rearrange("p a n -> p (a n)"),
-                                           in0=gates[h][g // 2][:, g % 2].rearrange("p a n -> p (a n)"), scalar=1.0,
-                                           in1=value_banks[g][:], op0=ALU.subtract, op1=ALU.mult)
+        def minus_one_times(dst, gate, factor):
+            nc.vector.scalar_tensor_tensor(
+                out=dst, in0=gate, scalar=1.0, in1=factor, op0=ALU.subtract, op1=ALU.mult
+            )
 
-        def join(h, pair, members):
-            nc.vector.scalar_tensor_tensor(out=grad[h][pair][:, members, :], in0=parts[h][pair][:, members, 0, :], scalar=0.125,
-                                           in1=parts[h][pair][:, members, 1, :], op0=ALU.mult, op1=ALU.mult)
+        def eighth_times(dst, a, b):
+            nc.vector.scalar_tensor_tensor(out=dst, in0=a, scalar=0.125, in1=b, op0=ALU.mult, op1=ALU.mult)
 
-        def add_old(engine, h, pair, members):
-            engine.tensor_tensor(out=res[h][pair][:, members, :], in0=grad[h][pair][:, members, :],
-                                 in1=prev[pair][:, members, halves[h]], op=ALU.add)
+        def times_z1(g):
+            minus_one_times(
+                parts[0][g // 2][:, g % 2, 0, :], gates[0][g // 2][:, g % 2, 0, :], value_banks[g][:, halves[0]]
+            )
+
+        def times_slope(pair):
+            minus_one_times(parts[0][pair][:, :, 1, :], gates[0][pair][:, :, 1, :], parts[0][pair][:, :, 0, :])
+
+        def times_c0(g):
+            eighth_times(grad[0][g // 2][:, g % 2, :], parts[0][g // 2][:, g % 2, 1, :], value_banks[g][:, halves[1]])
+
+        def gate_values(g):
+            minus_one_times(
+                parts[1][g // 2][:, g % 2].rearrange("p a n -> p (a n)"),
+                gates[1][g // 2][:, g % 2].rearrange("p a n -> p (a n)"),
+                value_banks[g][:],
+            )
+
+        def join(pair, members):
+            eighth_times(grad[1][pair][:, members, :], parts[1][pair][:, members, 0, :], parts[1][pair][:, members, 1, :])
+
+        def add_old_and_store(engine, h, pair, members):
+            engine.tensor_tensor(
+                out=res[h][pair][:, members, :],
+                in0=grad[h][pair][:, members, :],
+                in1=prev[pair][:, members, halves[h]],
+                op=ALU.add,
+            )
             dst = out[2 * pair : 2 * pair + 2].rearrange("g m n -> m g n")
             nc.sync.dma_start(out=dst[:, members, halves[h]], in_=res[h][pair][:, members, :])
 
-        both = slice(0, 2)
         v_copy = nc.vector.tensor_copy
 
         def s_copy(out, in_):
             nc.scalar.activation(out=out, in_=in_, func=ACT.Copy)
 
+        def z1(h, groups):
+            return [(value_banks, 0, "w1", "x%d" % h, g) for g in groups]
 
-        def across(banks, place, w_name, a_name):
-            for n0 in range(0, HALF, MM_N):
-                for g in range(G):
-                    product(banks, place, w_name, a_name, g, [n0])
+        def c0(h, groups):
+            return [(value_banks, 1, "wo", "dy%d" % h, g) for g in groups]
 
-        def gate_products(h, g):
-            product(gate_banks, 1, "w2", "x%d" % h, g, blocks)
-            product(gate_banks, 0, "w3", "x%d" % h, g, blocks)
+        def z3(h, groups):
+            return [(gate_banks, 0, "w3", "x%d" % h, g) for g in groups]
 
-        def value_products(h, g):
-            product(value_banks, 0, "w1", "x%d" % h, g, blocks)
-            product(value_banks, 1, "wo", "dy%d" % h, g, blocks)
+        def z2(h, groups):
+            return [(gate_banks, 1, "w2", "x%d" % h, g) for g in groups]
 
-        def times_z1(g):
-            nc.vector.scalar_tensor_tensor(out=parts[0][g // 2][:, g % 2, 0, :], in0=gates[0][g // 2][:, g % 2, 0, :], scalar=1.0,
-                                           in1=value_banks[g][:, halves[0]], op0=ALU.subtract, op1=ALU.mult)
+        every = range(G)
+        first, second, both = slice(0, 1), slice(1, 2), slice(0, 2)
 
-        def times_slope(pair):
-            nc.vector.scalar_tensor_tensor(out=parts[0][pair][:, :, 1, :], in0=gates[0][pair][:, :, 1, :], scalar=1.0,
-                                           in1=parts[0][pair][:, :, 0, :], op0=ALU.subtract, op1=ALU.mult)
-
-        def times_c0(g):
-            nc.vector.scalar_tensor_tensor(out=grad[0][g // 2][:, g % 2, :], in0=parts[0][g // 2][:, g % 2, 1, :], scalar=0.125,
-                                           in1=value_banks[g][:, halves[1]], op0=ALU.mult, op1=ALU.mult)
-
-        blocks = list(range(0, HALF, MM_N))
-        first, second = slice(0, 1), slice(1, 2)
         interleave(v_copy, "x0", "x", 0, 0, HALF)
         interleave(s_copy, "x1", "x", HALF, 0, HALF)
         interleave(v_copy, "w3", "w3", 0, 0, M)
         quantize("x0")
         quantize("w3")
-        across(gate_banks, 0, "w3", "x0")
+        multiply(z3(0, every))
         nc.vector.transpose(out=th_cols[:], in_=th_rows[:])
         interleave(s_copy, "w1", "w1", 0, 0, M)
         nc.scalar.activation(out=bias3[:], in_=th_cols[:, 0:P:ROWS], func=ACT.Copy, scale=0.5)
         quantize("x1")
         quantize("w1")
-        across(value_banks, 0, "w1", "x0")
+        multiply(z1(0, every))
         interleave(v_copy, "w2", "w2", 0, 0, M)
         quantize("w2")
-        for g in range(G):
-            tanh3(0, g)
-            product(gate_banks, 1, "w2", "x0", g, blocks)
-        for g in range(3):
+
+        for pair in range(2):
+            tanh3(0, 2 * pair)
+            tanh3(0, 2 * pair + 1)
+            multiply(z2(0, [2 * pair, 2 * pair + 1]))
+        for g in range(G - 1):
             times_z1(g)
             tanh2(0, g)
         square2(0, 0)
-        tanh2(0, 3)
+        tanh2(0, G - 1)
+        multiply(z2(1, range(G - 1)))
+        multiply(z3(1, range(G - 1)))
+
         interleave(v_copy, "dy0", "dy", 0, 0, HALF)
-        times_z1(3)
         interleave(v_copy, "wo", "wo", 0, 0, M)
         quantize("dy0")
         quantize("wo")
-        for g in range(3):
-            gate_products(1, g)
-        across(value_banks, 1, "wo", "dy0")
-        gate_products(1, 3)
+        times_z1(G - 1)
+        multiply(c0(0, every))
         interleave(s_copy, "dy1", "dy", HALF, 0, HALF // 2)
         square2(0, 1)
-        interleave(s_copy, "dy1", "dy", HALF, HALF // 2, 3 * HALF // 4)
+        interleave(s_copy, "dy1", "dy", HALF, HALF // 2, DY1_SPLIT)
         times_slope(0)
-        interleave(v_copy, "dy1", "dy", HALF, 3 * HALF // 4, HALF)
+        interleave(v_copy, "dy1", "dy", HALF, DY1_SPLIT, HALF)
+
         times_c0(0)
+        multiply(z2(1, [G - 1]) + z1(1, [0]))
         times_slope(1)
         quantize("dy1")
-        value_products(1, 0)
+        multiply(c0(1, [0]) + z3(1, [G - 1]))
         times_c0(1)
-        add_old(nc.gpsimd, 0, 0, both)
-        value_products(1, 1)
+        add_old_and_store(nc.gpsimd, 0, 0, both)
+        multiply(z1(1, [1]))
+        multiply(c0(1, [1]))
         times_c0(2)
         times_c0(3)
-        value_products(1, 2)
-        value_products(1, 3)
+        multiply(z1(1, [2, 3]))
+        multiply(c0(1, [2, 3]))
+
         for pair in range(2):
             tanh2(1, 2 * pair)
             tanh2(1, 2 * pair + 1)
             tanh3(1, 2 * pair)
             square2(1, pair)
             tanh3(1, 2 * pair + 1)
-        gate_values(1, 0)
-        add_old(nc.gpsimd, 0, 1, first)
-        gate_values(1, 1)
-        join(1, 0, first)
-        join(1, 0, second)
-        add_old(nc.vector, 0, 1, second)
-        add_old(nc.gpsimd, 1, 0, both)
-        gate_values(1, 2)
-        gate_values(1, 3)
-        join(1, 1, first)
-        join(1, 1, second)
-        add_old(nc.vector, 1, 1, first)
-        add_old(nc.vector, 1, 1, second)
+        gate_values(0)
+        add_old_and_store(nc.gpsimd, 0, 1, first)
+        gate_values(1)
+        join(0, first)
+        join(0, second)
+        add_old_and_store(nc.vector, 0, 1, second)
+        add_old_and_store(nc.gpsimd, 1, 0, both)
+        gate_values(2)
+        gate_values(3)
+        join(1, first)
+        join(1, second)
+        add_old_and_store(nc.vector, 1, 1, first)
+        add_old_and_store(nc.vector, 1, 1, second)

from contextlib import ExitStack

import concourse.mybir as mybir

G, D, M, N = 4, 128, 128, 512
FLOPS = 4 * 2 * G * D * M * N

F32 = mybir.dt.float32
BF16 = mybir.dt.bfloat16
U32 = mybir.dt.uint32
U8 = mybir.dt.uint8
FP8X4 = mybir.dt.float8_e4m3fn_x4
ACT = mybir.ActivationFunctionType
ALU = mybir.AluOpType

P = 128
PACK = 4
ROWS = D // PACK
HALF = N // 2
MM_N = 128
LINE = 4
DY1_SPLIT = 3 * HALF // 4


def tile_rows_btwogates_kernel(tc, x, w1, w2, w3, th, wo, dy, old, out):
    nc = tc.nc
    with ExitStack() as ctx:
        sb = ctx.enter_context(tc.tile_pool(name="sb", bufs=1))
        ps = ctx.enter_context(tc.psum_pool(name="ps", bufs=1))
        ctx.enter_context(tc.manual_schedule())

        raw, packed, codes, scales = {}, {}, {}, {}

        def load(name, src):
            raw[name] = sb.tile([P, PACK, src.shape[2]], F32, name="raw_" + name, align_bytes=64)
            nc.sync.dma_start(out=raw[name][:], in_=src.rearrange("g (p j) n -> (g p) j n", j=PACK))

        def operand(name, width):
            packed[name] = sb.tile([P, PACK * width], BF16, name="packed_" + name, align_bytes=64)
            codes[name] = sb.tile([P, width], U32, name="codes_" + name, align_bytes=64)
            scales[name] = sb.tile([P, width], U8, name="scales_" + name, align_bytes=64)

        def interleave(copy, name, src_name, src0, start, stop):
            dst = packed[name][:, PACK * start : PACK * stop].rearrange("p (c i j) -> p c j i", i=LINE, j=PACK)
            src = raw[src_name][:, :, src0 + start : src0 + stop].rearrange("p j (c i) -> p c j i", i=LINE)
            copy(out=dst, in_=src)

        def quantize(name):
            nc.vector.quantize_mx(out=codes[name][:].bitcast(FP8X4), scales=scales[name][:], in_=packed[name][:])

        def multiply(jobs):
            for n0 in range(0, HALF, MM_N):
                for banks, place, w_name, a_name, g in jobs:
                    rows = slice(ROWS * g, ROWS * (g + 1))
                    nc.tensor.matmul_mx(
                        out=banks[g][:, place * HALF + n0 : place * HALF + n0 + MM_N],
                        lhsT=codes[w_name][rows, :].bitcast(FP8X4),
                        lhsT_scale=scales[w_name][rows, :],
                        rhs=codes[a_name][rows, n0 : n0 + MM_N].bitcast(FP8X4),
                        rhs_scale=scales[a_name][rows, n0 : n0 + MM_N],
                        start=True,
                        stop=True,
                    )

        gate_banks = [ps.tile([P, N], F32, name="gate_bank%d" % g) for g in range(G)]
        value_banks = [ps.tile([P, N], F32, name="value_bank%d" % g) for g in range(G)]

        def work(name, shape):
            return [
                [sb.tile(shape, F32, name="%s%d%d" % (name, h, pair), align_bytes=64) for pair in range(2)]
                for h in range(2)
            ]

        t2 = work("t2", [P, 2, HALF])
        gates = work("gates", [P, 2, 2, HALF])
        parts = work("parts", [P, 2, 2, HALF])
        grad = work("grad", [P, 2, HALF])
        res = work("res", [P, 2, HALF])
        prev = [sb.tile([P, 2, N], F32, name="prev%d" % pair, align_bytes=64) for pair in range(2)]
        th_rows = sb.tile([P, P], F32, name="th_rows", align_bytes=64)
        th_cols = sb.tile([P, P], F32, name="th_cols", align_bytes=64)
        bias3 = sb.tile([P, G], F32, name="bias3")

        halves = [slice(0, HALF), slice(HALF, N)]

        nc.vector.memset(th_rows[:], 0.0)
        load("x", x)
        nc.sync.dma_start(
            out=th_rows[0:P:ROWS, :].rearrange("c (g i) -> c g i", g=G),
            in_=th.rearrange("g (c i) o -> c g (i o)", c=G),
        )
        load("w3", w3)
        load("w1", w1)
        load("w2", w2)
        load("dy", dy)
        load("wo", wo)
        for name in ("w1", "w2", "w3", "wo"):
            operand(name, M)
        for name in ("x0", "x1", "dy0", "dy1"):
            operand(name, HALF)
        for pair in range(2):
            nc.sync.dma_start(out=prev[pair][:], in_=old[2 * pair : 2 * pair + 2].rearrange("g m n -> m g n"))

        def tanh3(h, g):
            nc.scalar.activation(
                out=gates[h][g // 2][:, g % 2, 0, :],
                in_=gate_banks[g][:, halves[0]],
                func=ACT.Tanh,
                scale=-0.5,
                bias=bias3[:, g : g + 1],
            )

        def tanh2(h, g):
            nc.scalar.activation(
                out=t2[h][g // 2][:, g % 2, :], in_=gate_banks[g][:, halves[1]], func=ACT.Tanh, scale=0.5
            )

        def square2(h, pair):
            nc.scalar.activation(out=gates[h][pair][:, :, 1, :], in_=t2[h][pair][:], func=ACT.Square)

        def minus_one_times(dst, gate, factor):
            nc.vector.scalar_tensor_tensor(
                out=dst, in0=gate, scalar=1.0, in1=factor, op0=ALU.subtract, op1=ALU.mult
            )

        def eighth_times(dst, a, b):
            nc.vector.scalar_tensor_tensor(out=dst, in0=a, scalar=0.125, in1=b, op0=ALU.mult, op1=ALU.mult)

        def times_z1(g):
            minus_one_times(
                parts[0][g // 2][:, g % 2, 0, :], gates[0][g // 2][:, g % 2, 0, :], value_banks[g][:, halves[0]]
            )

        def times_slope(pair):
            minus_one_times(parts[0][pair][:, :, 1, :], gates[0][pair][:, :, 1, :], parts[0][pair][:, :, 0, :])

        def times_c0(g):
            eighth_times(grad[0][g // 2][:, g % 2, :], parts[0][g // 2][:, g % 2, 1, :], value_banks[g][:, halves[1]])

        def gate_values(g):
            minus_one_times(
                parts[1][g // 2][:, g % 2].rearrange("p a n -> p (a n)"),
                gates[1][g // 2][:, g % 2].rearrange("p a n -> p (a n)"),
                value_banks[g][:],
            )

        def join(pair, members):
            eighth_times(grad[1][pair][:, members, :], parts[1][pair][:, members, 0, :], parts[1][pair][:, members, 1, :])

        def add_old_and_store(engine, h, pair, members):
            engine.tensor_tensor(
                out=res[h][pair][:, members, :],
                in0=grad[h][pair][:, members, :],
                in1=prev[pair][:, members, halves[h]],
                op=ALU.add,
            )
            dst = out[2 * pair : 2 * pair + 2].rearrange("g m n -> m g n")
            nc.sync.dma_start(out=dst[:, members, halves[h]], in_=res[h][pair][:, members, :])

        v_copy = nc.vector.tensor_copy

        def s_copy(out, in_):
            nc.scalar.activation(out=out, in_=in_, func=ACT.Copy)

        def z1(h, groups):
            return [(value_banks, 0, "w1", "x%d" % h, g) for g in groups]

        def c0(h, groups):
            return [(value_banks, 1, "wo", "dy%d" % h, g) for g in groups]

        def z3(h, groups):
            return [(gate_banks, 0, "w3", "x%d" % h, g) for g in groups]

        def z2(h, groups):
            return [(gate_banks, 1, "w2", "x%d" % h, g) for g in groups]

        every = range(G)
        first, second, both = slice(0, 1), slice(1, 2), slice(0, 2)

        interleave(v_copy, "x0", "x", 0, 0, HALF)
        interleave(s_copy, "x1", "x", HALF, 0, HALF)
        interleave(v_copy, "w3", "w3", 0, 0, M)
        quantize("x0")
        quantize("w3")
        multiply(z3(0, every))
        nc.vector.transpose(out=th_cols[:], in_=th_rows[:])
        interleave(s_copy, "w1", "w1", 0, 0, M)
        nc.scalar.activation(out=bias3[:], in_=th_cols[:, 0:P:ROWS], func=ACT.Copy, scale=0.5)
        quantize("x1")
        quantize("w1")
        multiply(z1(0, every))
        interleave(v_copy, "w2", "w2", 0, 0, M)
        quantize("w2")

        for pair in range(2):
            tanh3(0, 2 * pair)
            tanh3(0, 2 * pair + 1)
            multiply(z2(0, [2 * pair, 2 * pair + 1]))
        for g in range(G - 1):
            times_z1(g)
            tanh2(0, g)
        square2(0, 0)
        tanh2(0, G - 1)
        multiply(z2(1, range(G - 1)))
        multiply(z3(1, range(G - 1)))

        interleave(v_copy, "dy0", "dy", 0, 0, HALF)
        interleave(v_copy, "wo", "wo", 0, 0, M)
        quantize("dy0")
        quantize("wo")
        times_z1(G - 1)
        multiply(c0(0, every))
        interleave(s_copy, "dy1", "dy", HALF, 0, HALF // 2)
        square2(0, 1)
        interleave(s_copy, "dy1", "dy", HALF, HALF // 2, DY1_SPLIT)
        times_slope(0)
        interleave(v_copy, "dy1", "dy", HALF, DY1_SPLIT, HALF)

        times_c0(0)
        multiply(z2(1, [G - 1]) + z1(1, [0]))
        times_slope(1)
        quantize("dy1")
        multiply(c0(1, [0]) + z3(1, [G - 1]))
        times_c0(1)
        add_old_and_store(nc.gpsimd, 0, 0, both)
        multiply(z1(1, [1]))
        multiply(c0(1, [1]))
        times_c0(2)
        times_c0(3)
        multiply(z1(1, [2, 3]))
        multiply(c0(1, [2, 3]))

        for pair in range(2):
            tanh2(1, 2 * pair)
            tanh2(1, 2 * pair + 1)
            tanh3(1, 2 * pair)
            square2(1, pair)
            tanh3(1, 2 * pair + 1)
        gate_values(0)
        add_old_and_store(nc.gpsimd, 0, 1, first)
        gate_values(1)
        join(0, first)
        join(0, second)
        add_old_and_store(nc.vector, 0, 1, second)
        add_old_and_store(nc.gpsimd, 1, 0, both)
        gate_values(2)
        gate_values(3)
        join(1, first)
        join(1, second)
        add_old_and_store(nc.vector, 1, 1, first)
        add_old_and_store(nc.vector, 1, 1, second)
